import numpy as np, ml_dtypes
CORES = [51,54,179,182]
N = 4
import mx_ref
NC, G = 256, 4
C = np.float32(0.031)
CNT = [[0,56,48,152],[88,0,120,48],[48,64,88,56],[120,136,0,0]]
OFF = [[sum(c[:e]) for e in range(N + 1)] for c in CNT]
BF = ml_dtypes.bfloat16
def cut(t, i, w=512):
    return t[:, w * i:w * i + w]
def tile(rs):
    return np.stack(rs, axis=2).reshape(128, -1).astype(BF)
def layer(w, X):
    out = []
    for i in range(G):
        for t in range(len(X)):
            p = mx_ref.matmul(mx_ref.quantize(cut(w, len(X) * i + t)), X[t])
            z = p if t == 0 else z + p
        out.append(z)
    return out
def act(Z):
    return [np.maximum(z, 0) * C for z in Z]
def setup_inputs(rng):
    def f(*shape):
        return mx_ref.flush((rng.standard_normal(shape, dtype=np.float32) * np.exp2(rng.integers(-2, 3, shape[:-1] + (1,)))).astype(BF))
    return {"x": f(N, 128, 4 * NC), "w1": f(N, 128, G * 512), "w2": f(N, 128, 512)}
def setup_inputs_blocks(rng):
    d = setup_inputs(rng)
    for k in ("x", "w1", "w2"): d[k] = mx_ref.spread(d[k], rng, 4)
    return d
def setup_inputs_wide(rng):
    d = setup_inputs(rng)
    for k in ("x", "w1", "w2"): d[k] = mx_ref.flush((d[k].astype(np.float32) * np.exp2(rng.integers(-8, 9, (N, 1, 1))).astype(np.float32)).astype(BF))
    return d
def setup_inputs_zeros(rng):
    d = setup_inputs(rng); v = d["x"].reshape(N, 128, -1, 4).copy()
    v[np.broadcast_to((rng.random((N, 1, v.shape[2], 1)) < 0.33), v.shape)] = 0
    d["x"] = v.reshape(d["x"].shape)
    return d
def reference(x, w1, w2):
    y = np.zeros((N, 128, NC), np.float32)
    for e in range(N):
        t = np.concatenate([x[j][:, 4 * OFF[j][e]:4 * OFF[j][e + 1]] for j in range(N)], axis=1)
        p = mx_ref.matmul(mx_ref.quantize(w2[e]), mx_ref.quantize(tile(act(layer(w1[e], [mx_ref.quantize(t)])))))
        y[e] = p
    return {"y": y}

@@ -1,0 +1,170 @@
+from concourse.mybir import dt, AluOpType, ActivationFunctionType
+
+NC = 256
+MINW = 128
+G = 4
+C = 0.031
+BLOCK = 16
+Q2COL = 176
+EMAX = 208
+
+ORDER = ((3, 2, 1), (2, 3, 0), (0, 1, 3), (1, 0))
+HEAD = ((3,), (2, 3), (0, 1), (1,))
+LATE = ((3,), (0, 2), (0,), (1, 2))
+
+SCRATCH = {
+    "xb": ("sbuf", [128, 4 * NC], "bfloat16"),
+    "wb": ("sbuf", [128, 512 * (G + 1)], "bfloat16"),
+    "xq": ("sbuf", [128, 320], "float8_e4m3fn_x4"),
+    "xs": ("sbuf", [128, 320], "uint8"),
+    "wq": ("sbuf", [128, 128 * (G + 1)], "float8_e4m3fn_x4"),
+    "ws": ("sbuf", [128, 128 * (G + 1)], "uint8"),
+    "bq": ("sbuf", [128, 320], "float8_e4m3fn_x4"),
+    "bs": ("sbuf", [128, 320], "uint8"),
+    "hE": ("sbuf", [128, 4 * EMAX], "bfloat16"),
+    "hL": ("sbuf", [128, 4 * MINW], "bfloat16"),
+    "hq": ("sbuf", [128, EMAX + MINW], "float8_e4m3fn_x4"),
+    "hs": ("sbuf", [128, EMAX + MINW], "uint8"),
+    "yb": ("sbuf", [128, NC], "float32"),
+    "ps": ("psum", [128, 512 * 8], "float32"),
+}
+SEMAPHORES = (["x1", "x2", "wl1", "wl2", "q1", "q2", "wqd", "arrE", "arrL", "sent", "st"]
+              + [s + p for p in "EL" for s in ("z0", "z1", "z2", "z3", "a", "hd", "p", "c")])
+
+
+def _bits(m):
+    return [k for k in range(m.bit_length()) if (m >> k) & 1]
+
+
+def _pack(ks):
+    return sum(1 << k for k in ks)
+
+
+def _widen(a, b):
+    if b - a >= MINW:
+        return a, b
+    return (a, a + MINW) if a + MINW <= NC else (b - MINW, b)
+
+
+def _sends(j, T, topo):
+    me = T.cores[j]
+
+    def near(d):
+        return topo.host(T.cores[d]) == topo.host(me) and topo.chip(T.cores[d]) == topo.chip(me)
+
+    far = [d for d in ORDER[j] if not near(d)]
+    fm = 0
+    for d in far:
+        fm |= topo.mask(me, T.cores[d])
+    a, b = _pack(_bits(fm)[0::2]), _pack(_bits(fm)[1::2])
+    out = [(far[0], 0, a), (far[0], 1, b), (far[1], 0, b)]
+    for d in ORDER[j]:
+        if near(d):
+            rest = _bits(topo.mask(me, T.cores[d]) & ~fm)
+            out += [(d, 0, _pack(rest[0::2])), (d, 1, _pack(rest[1::2]))]
+    out.append((far[1], 1, a))
+    return out
+
+
+def rank_program(g, core, T, topo):
+    r = T.rank_of(core)
+    if r is None:
+        return
+    S = T.sem
+    cnt = T.tables["CNT"]
+    n = len(cnt)
+    off = [[sum(c[:e]) for e in range(n + 1)] for c in cnt]
+    pos = [[sum(cnt[i][e] for i in range(j)) for j in range(n + 1)] for e in range(n)]
+    base = [(-pos[e][e]) % BLOCK if cnt[e][e] else 0 for e in range(n)]
+
+    ha, hb = min(off[r][d] for d in HEAD[r]), max(off[r][d + 1] for d in HEAD[r])
+    h0, h1 = _widen(ha, hb)
+    t0, t1 = _widen(hb, NC) if ha == 0 else _widen(0, ha)
+    l0, l1 = (h1, NC) if h0 == 0 else (0, h0)
+    if cnt[r][r]:
+        assert off[r][r] == t0 and pos[r][r + 1] == NC
+        buf2, pl2, col2 = T.bq, T.bs, base[r] + pos[r][r]
+    else:
+        buf2, pl2, col2 = T.xq, T.xs, Q2COL
+
+    g.sync.dma_start(T.xb[:, 4 * h0:4 * h1], T.x[:, 4 * h0:4 * h1]).then_inc(S.x1, 16)
+    g.scalar.dma_start(T.xb[:, 4 * l0:4 * l1], T.x[:, 4 * l0:4 * l1]).then_inc(S.x2, 16)
+    g.sync.dma_start(T.wb[:, 0:512 * G], T.w1[:, :]).then_inc(S.wl1, 16)
+    g.scalar.dma_start(T.wb[:, 512 * G:512 * (G + 1)], T.w2[:, :]).then_inc(S.wl2, 16)
+
+    v = g.vector
+    v.wait_ge(S.x1, 16)
+    v.quantize_mx(T.xq[:, 0:h1 - h0], T.xs[:, 0:h1 - h0], T.xb[:, 4 * h0:4 * h1]).then_inc(S.q1, 1)
+    v.wait_ge(S.x2, 16)
+    v.quantize_mx(buf2[:, col2:col2 + t1 - t0], pl2[:, col2:col2 + t1 - t0], T.xb[:, 4 * t0:4 * t1]).then_inc(S.q2, 1)
+    v.wait_ge(S.wl1, 16)
+    v.quantize_mx(T.wq[:, 0:128 * G], T.ws[:, 0:128 * G], T.wb[:, 0:512 * G]).then_inc(S.wqd, 1)
+    v.wait_ge(S.wl2, 16)
+    v.quantize_mx(T.wq[:, 128 * G:128 * (G + 1)], T.ws[:, 128 * G:128 * (G + 1)],
+                  T.wb[:, 512 * G:512 * (G + 1)]).then_inc(S.wqd, 1)
+
+    waited, total = set(), 0
+    for d, plane, m in _sends(r, T, topo):
+        a, b = off[r][d], off[r][d + 1]
+        if h0 <= a and b <= h1:
+            cb, pb, col, sem = T.xq, T.xs, a - h0, "q1"
+        else:
+            cb, pb, col, sem = buf2, pl2, col2 + a - t0, "q2"
+        if sem not in waited:
+            g.wait_ge(S[sem], 1)
+            waited.add(sem)
+        c0 = base[d] + pos[d][r]
+        rid, pid = topo.addr(T.cores[d], core)
+        if plane:
+            out, src = T.bs[:, c0:c0 + b - a], pb[:, col:col + b - a]
+        else:
+            out, src = T.bq[:, c0:c0 + b - a].bitcast(dt.uint8), cb[:, col:col + b - a].bitcast(dt.uint8)
+        g.remote_dma(out, src, S.arrL if r in LATE[d] else S.arrE, S.sent, pid, rid, m)
+        total += len(_bits(m))
+    g.wait_ge(S.sent, total)
+
+    due = {"E": 0, "L": 0}
+    for j in range(n):
+        if j != r:
+            for d, plane, m in _sends(j, T, topo):
+                if d == r:
+                    due["L" if j in LATE[r] else "E"] += len(_bits(m))
+    la, lb = min(pos[r][j] for j in LATE[r]), max(pos[r][j + 1] for j in LATE[r])
+    ea, eb = (lb, NC) if la == 0 else (0, la)
+    assert (la == 0 or lb == NC) and eb - ea >= MINW
+
+    te = g.tensor
+    te.wait_ge(S.wqd, 2)
+    if cnt[r][r]:
+        te.wait_ge(S.q2, 1)
+    for p, (wa, wb), (ua, ub), bank, h, hc in (("E", (ea, eb), (ea, eb), 0, T.hE, 0),
+                                               ("L", _widen(la, lb), (la, lb), G, T.hL, EMAX)):
+        w = wb - wa
+        te.wait_ge(S["arr" + p], due[p])
+        for i in range(G):
+            te.matmul_mx(T.ps[:, 512 * (bank + i):512 * (bank + i) + w], T.wq[:, 128 * i:128 * i + 128],
+                         T.ws[:, 128 * i:128 * i + 128], T.bq[:, base[r] + wa:base[r] + wb],
+                         T.bs[:, base[r] + wa:base[r] + wb], True, True).then_inc(S["z%d" % i + p], 1)
+        for i in range(G):
+            z = T.ps[:, 512 * (bank + i):512 * (bank + i) + w]
+            if i % 2 == 0:
+                v.wait_ge(S["z%d" % i + p], 1)
+                v.tensor_scalar(h[:, i:4 * w:4], z, 0.0, C, AluOpType.max, AluOpType.mult).then_inc(S["a" + p], 1)
+            else:
+                g.scalar.wait_ge(S["z%d" % i + p], 1)
+                g.scalar.activation(h[:, i:4 * w:4], z, ActivationFunctionType.Relu, scale=C).then_inc(S["a" + p], 1)
+        v.wait_ge(S["a" + p], G)
+        v.quantize_mx(T.hq[:, hc:hc + w], T.hs[:, hc:hc + w], h[:, 0:4 * w]).then_inc(S["hd" + p], 1)
+        te.wait_ge(S["hd" + p], 1)
+        te.matmul_mx(T.ps[:, 512 * bank:512 * bank + w], T.wq[:, 128 * G:128 * G + 128], T.ws[:, 128 * G:128 * G + 128],
+                     T.hq[:, hc:hc + w], T.hs[:, hc:hc + w], True, True).then_inc(S["p" + p], 1)
+        res = T.ps[:, 512 * bank + ua - wa:512 * bank + ub - wa]
+        if p == "E":
+            g.scalar.wait_ge(S.pE, 1)
+            g.scalar.activation(T.yb[:, ua:ub], res, ActivationFunctionType.Copy).then_inc(S.cE, 1)
+        else:
+            v.wait_ge(S.pL, 1)
+            v.tensor_copy(T.yb[:, ua:ub], res).then_inc(S.cL, 1)
+        g.sync.wait_ge(S["c" + p], 1)
+        g.sync.dma_start(T.y[:, ua:ub], T.yb[:, ua:ub]).then_inc(S.st, 16)
+    g.sync.wait_ge(S.st, 32)

@@ -6,11 +6,13 @@ G = 4
 C = 0.031
 BLOCK = 16
 Q2COL = 176
-EMAX = 208
+EMAX = 160
+NEAR_AT = 3
 
 ORDER = ((3, 2, 1), (2, 3, 0), (0, 1, 3), (1, 0))
 HEAD = ((3,), (2, 3), (0, 1), (1,))
 LATE = ((3,), (0, 2), (0,), (1, 2))
+PARTS = "OEL"
 
 SCRATCH = {
     "xb": ("sbuf", [128, 4 * NC], "bfloat16"),
@@ -21,15 +23,16 @@ SCRATCH = {
     "ws": ("sbuf", [128, 128 * (G + 1)], "uint8"),
     "bq": ("sbuf", [128, 320], "float8_e4m3fn_x4"),
     "bs": ("sbuf", [128, 320], "uint8"),
+    "hO": ("sbuf", [128, 4 * EMAX], "bfloat16"),
     "hE": ("sbuf", [128, 4 * EMAX], "bfloat16"),
-    "hL": ("sbuf", [128, 4 * MINW], "bfloat16"),
-    "hq": ("sbuf", [128, EMAX + MINW], "float8_e4m3fn_x4"),
-    "hs": ("sbuf", [128, EMAX + MINW], "uint8"),
+    "hL": ("sbuf", [128, 4 * EMAX], "bfloat16"),
+    "hq": ("sbuf", [128, 3 * EMAX], "float8_e4m3fn_x4"),
+    "hs": ("sbuf", [128, 3 * EMAX], "uint8"),
     "yb": ("sbuf", [128, NC], "float32"),
     "ps": ("psum", [128, 512 * 8], "float32"),
 }
-SEMAPHORES = (["x1", "x2", "wl1", "wl2", "q1", "q2", "wqd", "arrE", "arrL", "sent", "st"]
-              + [s + p for p in "EL" for s in ("z0", "z1", "z2", "z3", "a", "hd", "p", "c")])
+SEMAPHORES = (["x1", "x2", "wl1", "wl2", "q1", "q2", "wq1", "wq2", "arrE", "arrL", "sent"]
+              + [s + p for p in PARTS for s in ("z0", "z1", "z2", "z3", "a", "hd", "p", "c", "s")])
 
 
 def _bits(m):
@@ -57,12 +60,11 @@ def _sends(j, T, topo):
     for d in far:
         fm |= topo.mask(me, T.cores[d])
     a, b = _pack(_bits(fm)[0::2]), _pack(_bits(fm)[1::2])
-    out = [(far[0], 0, a), (far[0], 1, b), (far[1], 0, b)]
+    out = [(far[0], 0, a), (far[0], 1, b), (far[1], 0, b), (far[1], 1, a)]
     for d in ORDER[j]:
         if near(d):
             rest = _bits(topo.mask(me, T.cores[d]) & ~fm)
-            out += [(d, 0, _pack(rest[0::2])), (d, 1, _pack(rest[1::2]))]
-    out.append((far[1], 1, a))
+            out[NEAR_AT:NEAR_AT] = [(d, 0, _pack(rest[0::2])), (d, 1, _pack(rest[1::2]))]
     return out
 
 
@@ -76,12 +78,13 @@ def rank_program(g, core, T, topo):
     off = [[sum(c[:e]) for e in range(n + 1)] for c in cnt]
     pos = [[sum(cnt[i][e] for i in range(j)) for j in range(n + 1)] for e in range(n)]
     base = [(-pos[e][e]) % BLOCK if cnt[e][e] else 0 for e in range(n)]
+    own = cnt[r][r]
 
     ha, hb = min(off[r][d] for d in HEAD[r]), max(off[r][d + 1] for d in HEAD[r])
     h0, h1 = _widen(ha, hb)
     t0, t1 = _widen(hb, NC) if ha == 0 else _widen(0, ha)
     l0, l1 = (h1, NC) if h0 == 0 else (0, h0)
-    if cnt[r][r]:
+    if own:
         assert off[r][r] == t0 and pos[r][r + 1] == NC
         buf2, pl2, col2 = T.bq, T.bs, base[r] + pos[r][r]
     else:
@@ -92,16 +95,16 @@ def rank_program(g, core, T, topo):
     g.sync.dma_start(T.wb[:, 0:512 * G], T.w1[:, :]).then_inc(S.wl1, 16)
     g.scalar.dma_start(T.wb[:, 512 * G:512 * (G + 1)], T.w2[:, :]).then_inc(S.wl2, 16)
 
-    v = g.vector
+    v, te, sc = g.vector, g.tensor, g.scalar
     v.wait_ge(S.x1, 16)
     v.quantize_mx(T.xq[:, 0:h1 - h0], T.xs[:, 0:h1 - h0], T.xb[:, 4 * h0:4 * h1]).then_inc(S.q1, 1)
     v.wait_ge(S.x2, 16)
     v.quantize_mx(buf2[:, col2:col2 + t1 - t0], pl2[:, col2:col2 + t1 - t0], T.xb[:, 4 * t0:4 * t1]).then_inc(S.q2, 1)
     v.wait_ge(S.wl1, 16)
-    v.quantize_mx(T.wq[:, 0:128 * G], T.ws[:, 0:128 * G], T.wb[:, 0:512 * G]).then_inc(S.wqd, 1)
+    v.quantize_mx(T.wq[:, 0:128 * G], T.ws[:, 0:128 * G], T.wb[:, 0:512 * G]).then_inc(S.wq1, 1)
     v.wait_ge(S.wl2, 16)
     v.quantize_mx(T.wq[:, 128 * G:128 * (G + 1)], T.ws[:, 128 * G:128 * (G + 1)],
-                  T.wb[:, 512 * G:512 * (G + 1)]).then_inc(S.wqd, 1)
+                  T.wb[:, 512 * G:512 * (G + 1)]).then_inc(S.wq2, 1)
 
     waited, total = set(), 0
     for d, plane, m in _sends(r, T, topo):
@@ -130,41 +133,63 @@ def rank_program(g, core, T, topo):
                 if d == r:
                     due["L" if j in LATE[r] else "E"] += len(_bits(m))
     la, lb = min(pos[r][j] for j in LATE[r]), max(pos[r][j + 1] for j in LATE[r])
-    ea, eb = (lb, NC) if la == 0 else (0, la)
-    assert (la == 0 or lb == NC) and eb - ea >= MINW
+    ea, eb = (lb, NC - own) if la == 0 else (0, la)
+    assert (la == 0 or lb == NC) and (la == 0 or not own)
+    plan = {"E": (_widen(ea, eb), (ea, eb), G), "L": (_widen(la, lb), (la, lb), 0)}
+    if own:
+        assert t1 - t0 >= MINW
+        plan["O"] = ((NC - own, NC - own + max(own, MINW)), (NC - own, NC), 0)
 
-    te = g.tensor
-    te.wait_ge(S.wqd, 2)
-    if cnt[r][r]:
-        te.wait_ge(S.q2, 1)
-    for p, (wa, wb), (ua, ub), bank, h, hc in (("E", (ea, eb), (ea, eb), 0, T.hE, 0),
-                                               ("L", _widen(la, lb), (la, lb), G, T.hL, EMAX)):
-        w = wb - wa
-        te.wait_ge(S["arr" + p], due[p])
+    def first(p):
+        (wa, wb), use, bank = plan[p]
+        w, h, hc = wb - wa, T["h" + p], EMAX * PARTS.index(p)
         for i in range(G):
             te.matmul_mx(T.ps[:, 512 * (bank + i):512 * (bank + i) + w], T.wq[:, 128 * i:128 * i + 128],
                          T.ws[:, 128 * i:128 * i + 128], T.bq[:, base[r] + wa:base[r] + wb],
                          T.bs[:, base[r] + wa:base[r] + wb], True, True).then_inc(S["z%d" % i + p], 1)
-        for i in range(G):
             z = T.ps[:, 512 * (bank + i):512 * (bank + i) + w]
             if i % 2 == 0:
                 v.wait_ge(S["z%d" % i + p], 1)
                 v.tensor_scalar(h[:, i:4 * w:4], z, 0.0, C, AluOpType.max, AluOpType.mult).then_inc(S["a" + p], 1)
             else:
-                g.scalar.wait_ge(S["z%d" % i + p], 1)
-                g.scalar.activation(h[:, i:4 * w:4], z, ActivationFunctionType.Relu, scale=C).then_inc(S["a" + p], 1)
+                sc.wait_ge(S["z%d" % i + p], 1)
+                sc.activation(h[:, i:4 * w:4], z, ActivationFunctionType.Relu, scale=C).then_inc(S["a" + p], 1)
         v.wait_ge(S["a" + p], G)
         v.quantize_mx(T.hq[:, hc:hc + w], T.hs[:, hc:hc + w], h[:, 0:4 * w]).then_inc(S["hd" + p], 1)
+
+    def second(p, on_vector, q):
+        (wa, wb), (ua, ub), bank = plan[p]
+        w, hc = wb - wa, EMAX * PARTS.index(p)
         te.wait_ge(S["hd" + p], 1)
         te.matmul_mx(T.ps[:, 512 * bank:512 * bank + w], T.wq[:, 128 * G:128 * G + 128], T.ws[:, 128 * G:128 * G + 128],
                      T.hq[:, hc:hc + w], T.hs[:, hc:hc + w], True, True).then_inc(S["p" + p], 1)
         res = T.ps[:, 512 * bank + ua - wa:512 * bank + ub - wa]
-        if p == "E":
-            g.scalar.wait_ge(S.pE, 1)
-            g.scalar.activation(T.yb[:, ua:ub], res, ActivationFunctionType.Copy).then_inc(S.cE, 1)
+        if on_vector:
+            v.wait_ge(S["p" + p], 1)
+            v.tensor_copy(T.yb[:, ua:ub], res).then_inc(S["c" + p], 1)
         else:
-            v.wait_ge(S.pL, 1)
-            v.tensor_copy(T.yb[:, ua:ub], res).then_inc(S.cL, 1)
-        g.sync.wait_ge(S["c" + p], 1)
-        g.sync.dma_start(T.y[:, ua:ub], T.yb[:, ua:ub]).then_inc(S.st, 16)
-    g.sync.wait_ge(S.st, 32)
+            sc.wait_ge(S["p" + p], 1)
+            sc.activation(T.yb[:, ua:ub], res, ActivationFunctionType.Copy).then_inc(S["c" + p], 1)
+        q.wait_ge(S["c" + p], 1)
+        q.dma_start(T.y[:, ua:ub], T.yb[:, ua:ub]).then_inc(S["s" + p], 16)
+
+    te.wait_ge(S.wq1, 1)
+    if own:
+        te.wait_ge(S.q2, 1)
+        first("O")
+        te.wait_ge(S.wq2, 1)
+        second("O", False, g.sync)
+    te.wait_ge(S.arrE, due["E"])
+    first("E")
+    te.wait_ge(S.arrL, due["L"])
+    if own:
+        te.wait_ge(S.cO, 1)
+    first("L")
+    if not own:
+        te.wait_ge(S.wq2, 1)
+    second("E", False, sc)
+    second("L", True, g.sync)
+    if own:
+        g.sync.wait_ge(S.sO, 16)
+    g.sync.wait_ge(S.sL, 16)
+    sc.wait_ge(S.sE, 16)

from concourse.mybir import dt, AluOpType, ActivationFunctionType

NC = 256
MINW = 128
G = 4
C = 0.031
BLOCK = 16
Q2COL = 176
EMAX = 160
NEAR_AT = 3

ORDER = ((3, 2, 1), (2, 3, 0), (0, 1, 3), (1, 0))
HEAD = ((3,), (2, 3), (0, 1), (1,))
LATE = ((3,), (0, 2), (0,), (1, 2))
PARTS = "OEL"

SCRATCH = {
    "xb": ("sbuf", [128, 4 * NC], "bfloat16"),
    "wb": ("sbuf", [128, 512 * (G + 1)], "bfloat16"),
    "xq": ("sbuf", [128, 320], "float8_e4m3fn_x4"),
    "xs": ("sbuf", [128, 320], "uint8"),
    "wq": ("sbuf", [128, 128 * (G + 1)], "float8_e4m3fn_x4"),
    "ws": ("sbuf", [128, 128 * (G + 1)], "uint8"),
    "bq": ("sbuf", [128, 320], "float8_e4m3fn_x4"),
    "bs": ("sbuf", [128, 320], "uint8"),
    "hO": ("sbuf", [128, 4 * EMAX], "bfloat16"),
    "hE": ("sbuf", [128, 4 * EMAX], "bfloat16"),
    "hL": ("sbuf", [128, 4 * EMAX], "bfloat16"),
    "hq": ("sbuf", [128, 3 * EMAX], "float8_e4m3fn_x4"),
    "hs": ("sbuf", [128, 3 * EMAX], "uint8"),
    "yb": ("sbuf", [128, NC], "float32"),
    "ps": ("psum", [128, 512 * 8], "float32"),
}
SEMAPHORES = (["x1", "x2", "wl1", "wl2", "q1", "q2", "wq1", "wq2", "arrE", "arrL", "sent"]
              + [s + p for p in PARTS for s in ("z0", "z1", "z2", "z3", "a", "hd", "p", "c", "s")])


def _bits(m):
    return [k for k in range(m.bit_length()) if (m >> k) & 1]


def _pack(ks):
    return sum(1 << k for k in ks)


def _widen(a, b):
    if b - a >= MINW:
        return a, b
    return (a, a + MINW) if a + MINW <= NC else (b - MINW, b)


def _sends(j, T, topo):
    me = T.cores[j]

    def near(d):
        return topo.host(T.cores[d]) == topo.host(me) and topo.chip(T.cores[d]) == topo.chip(me)

    far = [d for d in ORDER[j] if not near(d)]
    fm = 0
    for d in far:
        fm |= topo.mask(me, T.cores[d])
    a, b = _pack(_bits(fm)[0::2]), _pack(_bits(fm)[1::2])
    out = [(far[0], 0, a), (far[0], 1, b), (far[1], 0, b), (far[1], 1, a)]
    for d in ORDER[j]:
        if near(d):
            rest = _bits(topo.mask(me, T.cores[d]) & ~fm)
            out[NEAR_AT:NEAR_AT] = [(d, 0, _pack(rest[0::2])), (d, 1, _pack(rest[1::2]))]
    return out


def rank_program(g, core, T, topo):
    r = T.rank_of(core)
    if r is None:
        return
    S = T.sem
    cnt = T.tables["CNT"]
    n = len(cnt)
    off = [[sum(c[:e]) for e in range(n + 1)] for c in cnt]
    pos = [[sum(cnt[i][e] for i in range(j)) for j in range(n + 1)] for e in range(n)]
    base = [(-pos[e][e]) % BLOCK if cnt[e][e] else 0 for e in range(n)]
    own = cnt[r][r]

    ha, hb = min(off[r][d] for d in HEAD[r]), max(off[r][d + 1] for d in HEAD[r])
    h0, h1 = _widen(ha, hb)
    t0, t1 = _widen(hb, NC) if ha == 0 else _widen(0, ha)
    l0, l1 = (h1, NC) if h0 == 0 else (0, h0)
    if own:
        assert off[r][r] == t0 and pos[r][r + 1] == NC
        buf2, pl2, col2 = T.bq, T.bs, base[r] + pos[r][r]
    else:
        buf2, pl2, col2 = T.xq, T.xs, Q2COL

    g.sync.dma_start(T.xb[:, 4 * h0:4 * h1], T.x[:, 4 * h0:4 * h1]).then_inc(S.x1, 16)
    g.scalar.dma_start(T.xb[:, 4 * l0:4 * l1], T.x[:, 4 * l0:4 * l1]).then_inc(S.x2, 16)
    g.sync.dma_start(T.wb[:, 0:512 * G], T.w1[:, :]).then_inc(S.wl1, 16)
    g.scalar.dma_start(T.wb[:, 512 * G:512 * (G + 1)], T.w2[:, :]).then_inc(S.wl2, 16)

    v, te, sc = g.vector, g.tensor, g.scalar
    v.wait_ge(S.x1, 16)
    v.quantize_mx(T.xq[:, 0:h1 - h0], T.xs[:, 0:h1 - h0], T.xb[:, 4 * h0:4 * h1]).then_inc(S.q1, 1)
    v.wait_ge(S.x2, 16)
    v.quantize_mx(buf2[:, col2:col2 + t1 - t0], pl2[:, col2:col2 + t1 - t0], T.xb[:, 4 * t0:4 * t1]).then_inc(S.q2, 1)
    v.wait_ge(S.wl1, 16)
    v.quantize_mx(T.wq[:, 0:128 * G], T.ws[:, 0:128 * G], T.wb[:, 0:512 * G]).then_inc(S.wq1, 1)
    v.wait_ge(S.wl2, 16)
    v.quantize_mx(T.wq[:, 128 * G:128 * (G + 1)], T.ws[:, 128 * G:128 * (G + 1)],
                  T.wb[:, 512 * G:512 * (G + 1)]).then_inc(S.wq2, 1)

    waited, total = set(), 0
    for d, plane, m in _sends(r, T, topo):
        a, b = off[r][d], off[r][d + 1]
        if h0 <= a and b <= h1:
            cb, pb, col, sem = T.xq, T.xs, a - h0, "q1"
        else:
            cb, pb, col, sem = buf2, pl2, col2 + a - t0, "q2"
        if sem not in waited:
            g.wait_ge(S[sem], 1)
            waited.add(sem)
        c0 = base[d] + pos[d][r]
        rid, pid = topo.addr(T.cores[d], core)
        if plane:
            out, src = T.bs[:, c0:c0 + b - a], pb[:, col:col + b - a]
        else:
            out, src = T.bq[:, c0:c0 + b - a].bitcast(dt.uint8), cb[:, col:col + b - a].bitcast(dt.uint8)
        g.remote_dma(out, src, S.arrL if r in LATE[d] else S.arrE, S.sent, pid, rid, m)
        total += len(_bits(m))
    g.wait_ge(S.sent, total)

    due = {"E": 0, "L": 0}
    for j in range(n):
        if j != r:
            for d, plane, m in _sends(j, T, topo):
                if d == r:
                    due["L" if j in LATE[r] else "E"] += len(_bits(m))
    la, lb = min(pos[r][j] for j in LATE[r]), max(pos[r][j + 1] for j in LATE[r])
    ea, eb = (lb, NC - own) if la == 0 else (0, la)
    assert (la == 0 or lb == NC) and (la == 0 or not own)
    plan = {"E": (_widen(ea, eb), (ea, eb), G), "L": (_widen(la, lb), (la, lb), 0)}
    if own:
        assert t1 - t0 >= MINW
        plan["O"] = ((NC - own, NC - own + max(own, MINW)), (NC - own, NC), 0)

    def first(p):
        (wa, wb), use, bank = plan[p]
        w, h, hc = wb - wa, T["h" + p], EMAX * PARTS.index(p)
        for i in range(G):
            te.matmul_mx(T.ps[:, 512 * (bank + i):512 * (bank + i) + w], T.wq[:, 128 * i:128 * i + 128],
                         T.ws[:, 128 * i:128 * i + 128], T.bq[:, base[r] + wa:base[r] + wb],
                         T.bs[:, base[r] + wa:base[r] + wb], True, True).then_inc(S["z%d" % i + p], 1)
            z = T.ps[:, 512 * (bank + i):512 * (bank + i) + w]
            if i % 2 == 0:
                v.wait_ge(S["z%d" % i + p], 1)
                v.tensor_scalar(h[:, i:4 * w:4], z, 0.0, C, AluOpType.max, AluOpType.mult).then_inc(S["a" + p], 1)
            else:
                sc.wait_ge(S["z%d" % i + p], 1)
                sc.activation(h[:, i:4 * w:4], z, ActivationFunctionType.Relu, scale=C).then_inc(S["a" + p], 1)
        v.wait_ge(S["a" + p], G)
        v.quantize_mx(T.hq[:, hc:hc + w], T.hs[:, hc:hc + w], h[:, 0:4 * w]).then_inc(S["hd" + p], 1)

    def second(p, on_vector, q):
        (wa, wb), (ua, ub), bank = plan[p]
        w, hc = wb - wa, EMAX * PARTS.index(p)
        te.wait_ge(S["hd" + p], 1)
        te.matmul_mx(T.ps[:, 512 * bank:512 * bank + w], T.wq[:, 128 * G:128 * G + 128], T.ws[:, 128 * G:128 * G + 128],
                     T.hq[:, hc:hc + w], T.hs[:, hc:hc + w], True, True).then_inc(S["p" + p], 1)
        res = T.ps[:, 512 * bank + ua - wa:512 * bank + ub - wa]
        if on_vector:
            v.wait_ge(S["p" + p], 1)
            v.tensor_copy(T.yb[:, ua:ub], res).then_inc(S["c" + p], 1)
        else:
            sc.wait_ge(S["p" + p], 1)
            sc.activation(T.yb[:, ua:ub], res, ActivationFunctionType.Copy).then_inc(S["c" + p], 1)
        q.wait_ge(S["c" + p], 1)
        q.dma_start(T.y[:, ua:ub], T.yb[:, ua:ub]).then_inc(S["s" + p], 16)

    te.wait_ge(S.wq1, 1)
    if own:
        te.wait_ge(S.q2, 1)
        first("O")
        te.wait_ge(S.wq2, 1)
        second("O", False, g.sync)
    te.wait_ge(S.arrE, due["E"])
    first("E")
    te.wait_ge(S.arrL, due["L"])
    if own:
        te.wait_ge(S.cO, 1)
    first("L")
    if not own:
        te.wait_ge(S.wq2, 1)
    second("E", False, sc)
    second("L", True, g.sync)
    if own:
        g.sync.wait_ge(S.sO, 16)
    g.sync.wait_ge(S.sL, 16)
    sc.wait_ge(S.sE, 16)
